import numpy as np
import ml_dtypes


def mxq(x, axis, fmt="e4m3"):
    dtype, down = {"e4m3": (ml_dtypes.float8_e4m3fn, 7), "e5m2": (ml_dtypes.float8_e5m2, 14)}[fmt]
    v = np.moveaxis(np.asarray(x, np.float32).astype(ml_dtypes.bfloat16).astype(np.float64), axis, -1)
    blocks = v.reshape(v.shape[:-1] + (-1, 32))
    amax = np.abs(blocks).max(-1, keepdims=True)
    byte = np.maximum(np.where(amax > 0, np.frexp(amax)[1] - 1 + 127, 0) - down, 1)
    scale = np.exp2(byte - 127.0)
    codes = (blocks / scale).astype(np.float32).astype(dtype).astype(np.float64)
    return np.moveaxis((codes * scale).reshape(v.shape), -1, axis)


WIDE = False


def mx_kscale(k):
    if not WIDE:
        return np.ones(k)
    levels = np.array([10, -10, 5, -5, 0])
    if k % 512:
        return np.exp2(np.random.permutation(np.resize(levels, k // 32))).repeat(32)
    a = np.empty((k // 512, 16))
    for p in range(k // 512):
        a[p, :8] = np.random.permutation(np.resize(levels, 8))
        for g in range(8):
            far = levels[np.abs(levels - a[p, g]) >= 10]
            a[p, g + 8] = far[np.random.randint(len(far))]
    return np.exp2(a.ravel()).repeat(32)


def f64(x):
    return np.asarray(x).astype(np.float64)


def striped(idx):
    return np.tile(np.asarray(idx).reshape(-1, 16).T, (8, 1)).astype(np.uint16)


def unstriped(offs):
    return offs[:16].T.reshape(-1).astype(np.int64)


E2M1 = np.array([0.0, 0.5, 1.0, 1.5, 2.0, 3.0, 4.0, 6.0, -0.0, -0.5, -1.0, -1.5, -2.0, -3.0, -4.0, -6.0])


def pack_weight(w, fmt):
    k, n = w.shape
    w = f64(np.asarray(w, np.float32).astype(ml_dtypes.bfloat16)).reshape(k // 32, 32, n)
    amax = np.abs(w).max(1)
    if fmt == "e4m3":
        byte = np.frexp(amax)[1] - 1 + 127 - 7
    else:
        mant, ex = np.frexp(amax / 6.0)
        byte = np.where(mant > 0.5, ex, ex - 1) + 127
    byte = np.clip(np.where(amax > 0, byte, 1), 1, 254)
    scaled = (w * np.exp2(127.0 - byte)[:, None, :]).reshape(k, n).astype(np.float32)
    by_word = np.ascontiguousarray(scaled.reshape(k // 512, 128, 4, n).transpose(0, 1, 3, 2))
    if fmt == "e4m3":
        words = by_word.astype(ml_dtypes.float8_e4m3fn).view(np.uint8)
    else:
        c = by_word.astype(ml_dtypes.float4_e2m1fn).view(np.uint8) & 0xF
        words = (c[..., 0::2] | (c[..., 1::2] << 4)).reshape(k // 512, 128, 2 * n)
    return np.ascontiguousarray(words), np.ascontiguousarray(byte.astype(np.uint8).reshape(k // 512, 16, n))


def unpack_weight(words, scales, fmt):
    g, _, n = scales.shape
    words = np.ascontiguousarray(words).reshape(g, 128, n, -1)
    if fmt == "e4m3":
        vals = words.view(ml_dtypes.float8_e4m3fn).astype(np.float64)
    else:
        nib = np.empty((g, 128, n, 4), np.uint8)
        nib[..., 0::2] = words & 0xF
        nib[..., 1::2] = words >> 4
        vals = E2M1[nib]
    vals = vals * np.repeat(np.exp2(scales.astype(np.float64) - 127.0), 8, axis=1)[..., None]
    return vals.transpose(0, 1, 3, 2).reshape(g * 512, n)


def sigmoid(v):
    return 1.0 / (1.0 + np.exp(-v))


D, T, I, Q, E, V = 512, 2048, 512, 256, 512, 32


def setup_inputs():
    n = np.random.standard_normal
    idx = np.random.permutation(T)[:I]
    fd = mx_kscale(D)
    fi = mx_kscale(I)
    ti = np.ones(T)
    ti[idx] = fi
    keysp = pack_weight(n((D, T)) / fd[:, None], "e4m3")
    return {
        "query": (n((D, Q)) * 1.0 / np.sqrt(D) * fd[:, None]).astype(np.float32),
        "keys_words": keysp[0],
        "keys_scales": keysp[1],
        "lam": (np.random.uniform(0.3, 0.8, (1, Q))).astype(np.float32),
        "eager": (np.random.uniform(0.8, 2.0, (Q, 1))).astype(np.float32),
        "thresh": (np.random.uniform(1.5, 4.0, (Q, 1))).astype(np.float32),
        "os": (np.random.uniform(4.0, 16.0, (1, I)) * fi).astype(np.float32),
        "vals": (n((E, T)) / ti).astype(np.float32),
        "memq": (np.random.uniform(0.3, 1.0, (1, Q))).astype(np.float32),
        "offs": striped(idx),
    }


def reference(query, keys_words, keys_scales, lam, eager, thresh, os, vals, memq, offs):
    idx = unstriped(offs)
    keysu = unpack_weight(keys_words, keys_scales, "e4m3")
    keysidxg = keysu[:, idx]
    queryq = mxq(f64(query), 0, "e4m3")
    a0 = keysidxg.T @ queryq
    ag = a0.reshape(I, V, Q // V).max(axis=2)
    ar = np.repeat(ag, Q // V, axis=1)
    s0 = a0 - ar * f64(lam)
    s = s0.T
    m0 = np.max(s, axis=1, keepdims=True)
    m1 = np.mean(s, axis=1, keepdims=True)
    p = np.exp(s - m0)
    gt0 = sigmoid((m0 - m1) * f64(eager) - f64(thresh))
    w = p / np.sum(p, axis=1, keepdims=True) * gt0
    wo1 = w * f64(os)
    wt1 = wo1.T
    vt1 = f64(vals)[:, idx].T
    vt1q = mxq(vt1, 0, "e4m3")
    wt1q = mxq(wt1, 0, "e4m3")
    o = vt1q.T @ wt1q
    o1 = np.pad(o, ((0, 0), (1, 0)))[:, :Q]
    y = o - o1 * f64(memq)
    return y

@@ -1,0 +1,243 @@
+from contextlib import ExitStack
+
+import concourse.mybir as mybir
+from concourse.masks import make_identity
+
+D, T, I, Q, E, V = 512, 2048, 512, 256, 512, 32
+P = 128
+R = Q // V
+FLOPS = 2 * D * I * Q + 2 * I * E * Q
+
+F32 = mybir.dt.float32
+BF16 = mybir.dt.bfloat16
+I32 = mybir.dt.int32
+U32 = mybir.dt.uint32
+U16 = mybir.dt.uint16
+U8 = mybir.dt.uint8
+FP8X4 = mybir.dt.float8_e4m3fn_x4
+ALU = mybir.AluOpType
+ACT = mybir.ActivationFunctionType
+AX = mybir.AxisListType
+
+
+def tile_attend_groupbest_abstaining_rowchanges_kernel(
+    tc, query, keys_words, keys_scales, lam, eager, thresh, slot_factor, vals, memq, offs, out
+):
+    nc = tc.nc
+    with ExitStack() as ctx:
+        sb = ctx.enter_context(tc.tile_pool(name="sb", bufs=1))
+        reuse = ctx.enter_context(tc.tile_pool(name="reuse", bufs=1))
+        ps = ctx.enter_context(tc.psum_pool(name="ps", bufs=1))
+
+        def bank(k, shape, name):
+            return ps.tile(shape, F32, name=name, tag="bank%d" % k)
+
+        ks_pool = sb.tile([P, T], U8, name="ks_pool")
+        nc.vector.memset(ks_pool[:].bitcast(I32), 0)
+        ident = sb.tile([P, P], F32, name="ident")
+        make_identity(nc, ident[:])
+        lines = sb.tile([P, P], F32, name="lines")
+        nc.gpsimd.memset(lines[:], 0.0)
+
+        offsets = sb.tile([P, I // 16], U16, name="offsets")
+        nc.sync.dma_start(offsets[:], offs)
+        q_raw = sb.tile([P, 4, Q], F32, name="q_raw")
+        nc.sync.dma_start(out=q_raw[:], in_=query.rearrange("(p t) q -> p t q", t=4))
+        ks_rows = sb.tile([P, T // 4], I32, name="ks_rows")
+        for g in range(4):
+            rows = slice(32 * g, 32 * g + 4)
+            nc.sync.dma_start(out=ks_rows[rows, :], in_=keys_scales[0, 4 * g : 4 * g + 4, :].bitcast(I32))
+            nc.vector.tensor_copy(out=ks_pool[rows, :].bitcast(I32), in_=ks_rows[rows, :])
+        k_pool = sb.tile([P, T], U32, name="k_pool")
+        nc.sync.dma_start(out=k_pool[:].bitcast(I32), in_=keys_words[0].rearrange("p n t -> p (n t)").bitcast(I32))
+        lam_col = sb.tile([P, 2], F32, name="lam_col")
+        with nc.allow_non_contiguous_dma(reason="one value of lam to each partition"):
+            nc.sync.dma_start(out=lam_col[:], in_=lam.rearrange("o (j p) -> p (o j)", p=P))
+
+        def after_values(k, shape, dtype, name, at=0):
+            return reuse.tile(shape, dtype, name=name, offset=4 * T * k + at, align_bytes=64)
+
+        v_pool = [after_values(k, [P, T], F32, "v_pool%d" % k) for k in range(4)]
+        nc.sync.dma_start(out=v_pool[0][:], in_=vals[0:P, :])
+        nc.sync.dma_start(out=lines[0:4, :], in_=slot_factor.rearrange("o (c p) -> (o c) p", p=P))
+        nc.sync.dma_start(out=lines[4:6, :], in_=memq.rearrange("o (j p) -> (o j) p", p=P))
+        nc.sync.dma_start(out=lines[6:8, :], in_=eager.rearrange("(j p) o -> j (p o)", p=P))
+        nc.sync.dma_start(out=lines[8:10, :], in_=thresh.rearrange("(j p) o -> j (p o)", p=P))
+        for k in range(1, 4):
+            nc.sync.dma_start(out=v_pool[k][:], in_=vals[k * P : (k + 1) * P, :])
+
+        def columns(src, n, k, name):
+            turned = bank(k, [P, P], name + "_ps")
+            nc.tensor.transpose(turned[:], src[:], ident[:])
+            col = sb.tile([P, n], F32, name=name)
+            nc.scalar.activation(out=col[:], in_=turned[:, 0:n], func=ACT.Copy)
+            return col
+
+        def spread(dst, col, n):
+            for j in range(n):
+                nc.tensor.transpose(dst[:, j * P : (j + 1) * P], col[:, j : j + 1].to_broadcast([P, P]), ident[:])
+
+
+        q_bf = sb.tile([P, Q, 4], BF16, name="q_bf", align_bytes=64)
+        nc.scalar.activation(out=q_bf[:], in_=q_raw[:].rearrange("p t q -> p q t"), func=ACT.Copy)
+        q_codes = sb.tile([P, Q], U32, name="q_codes", align_bytes=64)
+        q_scales = sb.tile([P, Q], U8, name="q_scales", align_bytes=64)
+        nc.vector.quantize_mx(out=q_codes[:].bitcast(FP8X4), scales=q_scales[:], in_=q_bf[:].rearrange("p q t -> p (q t)"))
+
+        ks = sb.tile([P, I], U8, name="ks", align_bytes=64)
+        nc.vector.tensor_copy(out=ks[:], in_=ks_pool[:].indirect(offsets[:]))
+        kw = []
+        for b in range(2):
+            w = sb.tile([P, 2 * P], U32, name="kw%d" % b, align_bytes=64)
+            nc.vector.tensor_copy(out=w[:], in_=k_pool[:].indirect(offsets[:, 16 * b : 16 * (b + 1)]))
+            kw.append(w)
+
+        a_ps = []
+        for c in range(4):
+            acc = bank(c, [P, Q], "a_ps%d" % c)
+            nc.tensor.matmul_mx(
+                out=acc[:],
+                lhsT=kw[c // 2][:, (c % 2) * P : (c % 2 + 1) * P].bitcast(FP8X4),
+                lhsT_scale=ks[:, c * P : (c + 1) * P],
+                rhs=q_codes[:].bitcast(FP8X4),
+                rhs_scale=q_scales[:],
+                start=True,
+                stop=True,
+            )
+            a_ps.append(acc)
+        lam_row = bank(6, [P, Q], "lam_row")
+        spread(lam_row, lam_col, 2)
+        a_sb = []
+        neg_best = sb.tile([P, 4, V], F32, name="neg_best")
+        for c in range(4):
+            nc.vector.tensor_reduce(
+                out=neg_best[:, c, :], in_=a_ps[c][:].rearrange("p (v r) -> p v r", r=R), axis=AX.X, op=ALU.max, negate=True
+            )
+            a = sb.tile([P, Q], F32, name="a_sb%d" % c)
+            nc.scalar.copy(out=a[:], in_=a_ps[c][:])
+            a_sb.append(a)
+        VJ = V // 2
+        t_sb = []
+        for j in range(2):
+            t = sb.tile([P, 4, P], F32, name="t_sb%d" % j)
+            nc.vector.tensor_tensor(
+                out=t[:].rearrange("p c (v r) -> p c v r", r=R),
+                in0=neg_best[:, :, j * VJ : (j + 1) * VJ].unsqueeze(3).to_broadcast([P, 4, VJ, R]),
+                in1=lam_row[:, j * P : (j + 1) * P].rearrange("p (v r) -> p v r", r=R).unsqueeze(1).to_broadcast([P, 4, VJ, R]),
+                op=ALU.mult,
+            )
+            t_sb.append(t)
+
+        s_ps = [bank(4 + j, [P, I], "s_ps%d" % j) for j in range(2)]
+
+        def turn(c, j, src, start, stop):
+            nc.tensor.matmul(s_ps[j][:, c * P : (c + 1) * P], src, ident[:], start=start, stop=stop, is_transpose=True)
+
+        for j in range(2):
+            for c in range(4):
+                turn(c, j, a_sb[c][:, j * P : (j + 1) * P], c == 0, False)
+            for c in range(4):
+                turn(c, j, t_sb[j][:, c, :], False, c == 3)
+
+        cols = columns(lines, 10, 7, "cols")
+        os_col, memq_col, eager_col, thresh_col = cols[:, 0:4], cols[:, 4:6], cols[:, 6:8], cols[:, 8:10]
+        os_row = bank(7, [P, I], "os_row")
+        spread(os_row, os_col, 4)
+
+        def gather_values(k, tag):
+            g_bf = sb.tile([P, I], BF16, name="g_bf%d" % k, tag=tag, align_bytes=64)
+            nc.vector.tensor_copy(out=g_bf[:], in_=v_pool[k][:].indirect(offsets[:]))
+            return g_bf
+
+        def turn_pairs(src_bf, psum_tile, dst_bf):
+            words = src_bf.bitcast(F32)
+            for u in range(2):
+                nc.tensor.transpose(psum_tile[:, u, :], words[:, u : 2 * P : 2], ident[:])
+            nc.scalar.copy(out=dst_bf.bitcast(F32).rearrange("p (x u) -> p x u", u=2), in_=psum_tile[:].rearrange("p u x -> p x u"))
+
+        def turn_values(k, g_bf):
+            vt_bf = sb.tile([P, 4 * P], BF16, name="vt_bf%d" % k, align_bytes=64)
+            turn_pairs(g_bf[:], bank(2 + k % 2, [P, 2, P], "vt_ps%d" % k), vt_bf[:])
+            return vt_bf
+
+        memq_ps = bank(6, [P, Q], "memq_ps")
+        spread(memq_ps, memq_col, 2)
+        memq_row = sb.tile([P, Q], F32, name="memq_row")
+        nc.scalar.copy(out=memq_row[:], in_=memq_ps[:])
+
+        gathered = [gather_values(0, "g0")]
+
+        p_sb, by_scalar = [], []
+        for j in range(2):
+            p = sb.tile([P, I], F32, name="p_sb%d" % j, tag="p%d" % j, align_bytes=64)
+            st = sb.tile([P, 3], F32, name="by_scalar%d" % j)
+            nc.scalar.activation(out=p[:], in_=s_ps[j][:], func=ACT.Copy, scale=1.0 / I, accum_out=st[:, 0:1])
+            p_sb.append(p)
+            by_scalar.append(st)
+        row_max = after_values(0, [P, 4], F32, "row_max")
+        for j in range(2):
+            mean, p_sum, odds = [by_scalar[j][:, n : n + 1] for n in range(3)]
+            neg_max, logit = row_max[:, j : j + 1], row_max[:, 2 + j : 3 + j]
+            nc.vector.tensor_reduce(out=neg_max, in_=s_ps[j][:], axis=AX.X, op=ALU.max, negate=True)
+            nc.scalar.activation(out=p_sb[j][:], in_=s_ps[j][:], func=ACT.Exp, bias=neg_max, scale=1.0, accum_out=p_sum)
+            nc.vector.tensor_scalar(
+                out=logit, in0=mean, scalar1=neg_max, scalar2=eager_col[:, j : j + 1], op0=ALU.add, op1=ALU.mult
+            )
+            nc.scalar.activation(out=odds, in_=logit, func=ACT.Exp, bias=thresh_col[:, j : j + 1], scale=1.0)
+        gathered.append(gather_values(1, "g1"))
+        turned = [turn_values(k, gathered[k]) for k in range(2)]
+
+        row_factor = after_values(1, [P, 4], F32, "row_factor")
+        wt_bf = []
+        for j in range(2):
+            mean, p_sum, odds = [by_scalar[j][:, n : n + 1] for n in range(3)]
+            denom, factor = row_factor[:, j : j + 1], row_factor[:, 2 + j : 3 + j]
+            nc.vector.tensor_scalar(out=denom, in0=odds, scalar1=1.0, scalar2=p_sum, op0=ALU.add, op1=ALU.mult)
+            nc.vector.reciprocal(out=factor, in_=denom)
+            w_bf = sb.tile([P, I], BF16, name="w_bf%d" % j)
+            nc.vector.scalar_tensor_tensor(
+                out=w_bf[:], in0=p_sb[j][:], scalar=factor, in1=os_row[:], op0=ALU.mult, op1=ALU.mult
+            )
+            wt = sb.tile([P, 4 * P], BF16, name="wt_bf%d" % j, tag="wt%d" % j, align_bytes=64)
+            turn_pairs(w_bf[:], bank(j, [P, 2, P], "wt_ps%d" % j), wt[:])
+            wt_bf.append(wt)
+        gathered.append(gather_values(2, "p1"))
+        turned.append(turn_values(2, gathered[2]))
+        w_codes = after_values(2, [P, Q], U32, "w_codes")
+        w_scales = sb.tile([P, Q], U8, name="w_scales", align_bytes=64)
+        for j in range(2):
+            qs = slice(j * P, (j + 1) * P)
+            nc.vector.quantize_mx(out=w_codes[:, qs].bitcast(FP8X4), scales=w_scales[:, qs], in_=wt_bf[j][:])
+
+        def product(k, v_codes):
+            v_scales = sb.tile([P, P], U8, name="v_scales%d" % k, align_bytes=64)
+            nc.vector.quantize_mx(out=v_codes[:].bitcast(FP8X4), scales=v_scales[:], in_=turned[k][:])
+            o_ps = bank(4 + k, [P, Q], "o_ps%d" % k)
+            nc.tensor.matmul_mx(
+                out=o_ps[:],
+                lhsT=v_codes[:].bitcast(FP8X4),
+                lhsT_scale=v_scales[:],
+                rhs=w_codes[:].bitcast(FP8X4),
+                rhs_scale=w_scales[:],
+                start=True,
+                stop=True,
+            )
+            return o_ps
+
+        def differences(k, o_ps):
+            y = y_all[:, k, :]
+            nc.vector.tensor_tensor(out=y[:, 1:Q], in0=o_ps[:, 0 : Q - 1], in1=memq_row[:, 1:Q], op=ALU.mult)
+            nc.vector.tensor_tensor(out=y, in0=o_ps[:], in1=y, op=ALU.subtract)
+            nc.sync.dma_start(out=out[k * P : (k + 1) * P, :], in_=y)
+
+        sums = [product(k, sb.tile([P, P], U32, name="v_codes%d" % k, align_bytes=64)) for k in range(2)]
+        gathered.append(gather_values(3, "wt1"))
+        turned.append(turn_values(3, gathered[3]))
+        y_all = after_values(3, [P, 4, Q], F32, "y_all")
+        nc.vector.memset(y_all[:, :, 0:1], 0.0)
+        sums.append(product(2, after_values(3, [P, P], U32, "v_codes2", at=16 * Q)))
+        differences(0, sums[0])
+        differences(1, sums[1])
+        sums.append(product(3, sb.tile([P, P], U32, name="v_codes3", align_bytes=64)))
+        differences(2, sums[2])
+        differences(3, sums[3])

@@ -57,13 +57,15 @@ def tile_attend_groupbest_abstaining_rowchanges_kernel(
         def after_values(k, shape, dtype, name, at=0):
             return reuse.tile(shape, dtype, name=name, offset=4 * T * k + at, align_bytes=64)
 
+        def shared(tag, shape, dtype, name):
+            return sb.tile(shape, dtype, name=name, tag=tag, align_bytes=64)
+
         v_pool = [after_values(k, [P, T], F32, "v_pool%d" % k) for k in range(4)]
-        nc.sync.dma_start(out=v_pool[0][:], in_=vals[0:P, :])
         nc.sync.dma_start(out=lines[0:4, :], in_=slot_factor.rearrange("o (c p) -> (o c) p", p=P))
         nc.sync.dma_start(out=lines[4:6, :], in_=memq.rearrange("o (j p) -> (o j) p", p=P))
         nc.sync.dma_start(out=lines[6:8, :], in_=eager.rearrange("(j p) o -> j (p o)", p=P))
         nc.sync.dma_start(out=lines[8:10, :], in_=thresh.rearrange("(j p) o -> j (p o)", p=P))
-        for k in range(1, 4):
+        for k in range(4):
             nc.sync.dma_start(out=v_pool[k][:], in_=vals[k * P : (k + 1) * P, :])
 
         def columns(src, n, k, name):
@@ -108,7 +110,7 @@ def tile_attend_groupbest_abstaining_rowchanges_kernel(
         lam_row = bank(6, [P, Q], "lam_row")
         spread(lam_row, lam_col, 2)
         a_sb = []
-        neg_best = sb.tile([P, 4, V], F32, name="neg_best")
+        neg_best = shared("g0", [P, 4, V], F32, "neg_best")
         for c in range(4):
             nc.vector.tensor_reduce(
                 out=neg_best[:, c, :], in_=a_ps[c][:].rearrange("p (v r) -> p v r", r=R), axis=AX.X, op=ALU.max, negate=True
@@ -141,11 +143,10 @@ def tile_attend_groupbest_abstaining_rowchanges_kernel(
 
         cols = columns(lines, 10, 7, "cols")
         os_col, memq_col, eager_col, thresh_col = cols[:, 0:4], cols[:, 4:6], cols[:, 6:8], cols[:, 8:10]
-        os_row = bank(7, [P, I], "os_row")
+        os_row = bank(6, [P, I], "os_row")
         spread(os_row, os_col, 4)
 
-        def gather_values(k, tag):
-            g_bf = sb.tile([P, I], BF16, name="g_bf%d" % k, tag=tag, align_bytes=64)
+        def gather_values(k, g_bf):
             nc.vector.tensor_copy(out=g_bf[:], in_=v_pool[k][:].indirect(offsets[:]))
             return g_bf
 
@@ -155,89 +156,104 @@ def tile_attend_groupbest_abstaining_rowchanges_kernel(
                 nc.tensor.transpose(psum_tile[:, u, :], words[:, u : 2 * P : 2], ident[:])
             nc.scalar.copy(out=dst_bf.bitcast(F32).rearrange("p (x u) -> p x u", u=2), in_=psum_tile[:].rearrange("p u x -> p x u"))
 
-        def turn_values(k, g_bf):
-            vt_bf = sb.tile([P, 4 * P], BF16, name="vt_bf%d" % k, align_bytes=64)
-            turn_pairs(g_bf[:], bank(2 + k % 2, [P, 2, P], "vt_ps%d" % k), vt_bf[:])
-            return vt_bf
+        g0_bf = gather_values(0, shared("g0", [P, I], BF16, "g0_bf"))
 
-        memq_ps = bank(6, [P, Q], "memq_ps")
-        spread(memq_ps, memq_col, 2)
-        memq_row = sb.tile([P, Q], F32, name="memq_row")
-        nc.scalar.copy(out=memq_row[:], in_=memq_ps[:])
-
-        gathered = [gather_values(0, "g0")]
-
-        p_sb, by_scalar = [], []
+        p_sb, shift = [], []
         for j in range(2):
-            p = sb.tile([P, I], F32, name="p_sb%d" % j, tag="p%d" % j, align_bytes=64)
-            st = sb.tile([P, 3], F32, name="by_scalar%d" % j)
-            nc.scalar.activation(out=p[:], in_=s_ps[j][:], func=ACT.Copy, scale=1.0 / I, accum_out=st[:, 0:1])
-            p_sb.append(p)
-            by_scalar.append(st)
-        row_max = after_values(0, [P, 4], F32, "row_max")
-        for j in range(2):
-            mean, p_sum, odds = [by_scalar[j][:, n : n + 1] for n in range(3)]
-            neg_max, logit = row_max[:, j : j + 1], row_max[:, 2 + j : 3 + j]
-            nc.vector.tensor_reduce(out=neg_max, in_=s_ps[j][:], axis=AX.X, op=ALU.max, negate=True)
-            nc.scalar.activation(out=p_sb[j][:], in_=s_ps[j][:], func=ACT.Exp, bias=neg_max, scale=1.0, accum_out=p_sum)
-            nc.vector.tensor_scalar(
-                out=logit, in0=mean, scalar1=neg_max, scalar2=eager_col[:, j : j + 1], op0=ALU.add, op1=ALU.mult
+            p = after_values(4, [P, I], F32, "p_sb%d" % j, at=4 * I * j)
+            mean = sb.tile([P, 1], F32, name="mean%d" % j)
+            nc.scalar.activation(out=p[:], in_=s_ps[j][:], func=ACT.Copy, scale=1.0 / I, accum_out=mean[:])
+            sh = shared("shift%d" % j, [P, 1], F32, "shift%d" % j)
+            nc.scalar.activation(
+                out=sh[:], in_=mean[:], func=ACT.Identity, scale=eager_col[:, j : j + 1], bias=thresh_col[:, j : j + 1]
             )
-            nc.scalar.activation(out=odds, in_=logit, func=ACT.Exp, bias=thresh_col[:, j : j + 1], scale=1.0)
-        gathered.append(gather_values(1, "g1"))
-        turned = [turn_values(k, gathered[k]) for k in range(2)]
+            p_sb.append(p)
+            shift.append(sh)
+        row_max = after_values(0, [P, 2], F32, "row_max")
+        denom = []
+        for j in range(2):
+            neg_max = row_max[:, j : j + 1]
+            nc.vector.tensor_reduce(out=neg_max, in_=s_ps[j][:], axis=AX.X, op=ALU.max, negate=True)
+            odds = shared("odds%d" % j, [P, 1], F32, "odds%d" % j)
+            nc.scalar.activation(out=odds[:], in_=neg_max, func=ACT.Exp, scale=eager_col[:, j : j + 1], bias=shift[j][:])
+            p_sum = sb.tile([P, 1], F32, name="p_sum%d" % j)
+            nc.scalar.activation(out=p_sb[j][:], in_=s_ps[j][:], func=ACT.Exp, bias=neg_max, scale=1.0, accum_out=p_sum[:])
+            d = sb.tile([P, 1], F32, name="denom%d" % j)
+            nc.scalar.activation(out=d[:], in_=odds[:], func=ACT.Identity, scale=p_sum[:], bias=p_sum[:])
+            denom.append(d)
+        g1_bf = gather_values(1, shared("shift0", [P, I], BF16, "g1_bf"))
+        vt01 = shared("odds1", [P, 2, I], BF16, "vt01")
+        for k, g_bf in enumerate((g0_bf, g1_bf)):
+            turn_pairs(g_bf[:], bank(2, [P, 2, P], "vt_ps%d" % k), vt01[:, k, :])
 
-        row_factor = after_values(1, [P, 4], F32, "row_factor")
+        row_factor = after_values(1, [P, 2], F32, "row_factor")
         wt_bf = []
         for j in range(2):
-            mean, p_sum, odds = [by_scalar[j][:, n : n + 1] for n in range(3)]
-            denom, factor = row_factor[:, j : j + 1], row_factor[:, 2 + j : 3 + j]
-            nc.vector.tensor_scalar(out=denom, in0=odds, scalar1=1.0, scalar2=p_sum, op0=ALU.add, op1=ALU.mult)
-            nc.vector.reciprocal(out=factor, in_=denom)
-            w_bf = sb.tile([P, I], BF16, name="w_bf%d" % j)
+            factor = row_factor[:, j : j + 1]
+            nc.vector.reciprocal(out=factor, in_=denom[j][:])
+            w_bf = shared("w%d" % j, [P, I], BF16, "w_bf%d" % j)
             nc.vector.scalar_tensor_tensor(
                 out=w_bf[:], in0=p_sb[j][:], scalar=factor, in1=os_row[:], op0=ALU.mult, op1=ALU.mult
             )
-            wt = sb.tile([P, 4 * P], BF16, name="wt_bf%d" % j, tag="wt%d" % j, align_bytes=64)
+            wt = sb.tile([P, I], BF16, name="wt_bf%d" % j, align_bytes=64)
             turn_pairs(w_bf[:], bank(j, [P, 2, P], "wt_ps%d" % j), wt[:])
             wt_bf.append(wt)
-        gathered.append(gather_values(2, "p1"))
-        turned.append(turn_values(2, gathered[2]))
-        w_codes = after_values(2, [P, Q], U32, "w_codes")
+        memq_ps = bank(5, [P, Q], "memq_ps")
+        spread(memq_ps, memq_col, 2)
+        memq_row = sb.tile([P, Q], F32, name="memq_row")
+        nc.scalar.copy(out=memq_row[:], in_=memq_ps[:])
+        vt_late = []
+        for k in (2, 3):
+            g_bf = gather_values(k, after_values(4, [P, I], BF16, "g%d_bf" % k, at=4 * I + 2 * I * (k - 2)))
+            vt = sb.tile([P, I], BF16, name="vt%d" % k, align_bytes=64)
+            turn_pairs(g_bf[:], bank(k - 2, [P, 2, P], "vt_ps%d" % k), vt[:])
+            vt_late.append(vt)
+
+        def quantise(src_bf, codes, name):
+            scales = sb.tile([P, codes.shape[1]], U8, name=name, align_bytes=64)
+            nc.vector.quantize_mx(out=codes.bitcast(FP8X4), scales=scales[:], in_=src_bf)
+            return codes, scales[:]
+
+        w_codes = after_values(3, [P, Q], U32, "w_codes")
         w_scales = sb.tile([P, Q], U8, name="w_scales", align_bytes=64)
         for j in range(2):
             qs = slice(j * P, (j + 1) * P)
             nc.vector.quantize_mx(out=w_codes[:, qs].bitcast(FP8X4), scales=w_scales[:, qs], in_=wt_bf[j][:])
 
-        def product(k, v_codes):
-            v_scales = sb.tile([P, P], U8, name="v_scales%d" % k, align_bytes=64)
-            nc.vector.quantize_mx(out=v_codes[:].bitcast(FP8X4), scales=v_scales[:], in_=turned[k][:])
-            o_ps = bank(4 + k, [P, Q], "o_ps%d" % k)
+        def product(o_ps, v_codes, v_scales):
             nc.tensor.matmul_mx(
-                out=o_ps[:],
-                lhsT=v_codes[:].bitcast(FP8X4),
-                lhsT_scale=v_scales[:],
+                out=o_ps,
+                lhsT=v_codes.bitcast(FP8X4),
+                lhsT_scale=v_scales,
                 rhs=w_codes[:].bitcast(FP8X4),
                 rhs_scale=w_scales[:],
                 start=True,
                 stop=True,
             )
-            return o_ps
 
-        def differences(k, o_ps):
-            y = y_all[:, k, :]
-            nc.vector.tensor_tensor(out=y[:, 1:Q], in0=o_ps[:, 0 : Q - 1], in1=memq_row[:, 1:Q], op=ALU.mult)
+        y_all = sb.tile([P, 4, Q], F32, name="y_all")
+        nc.gpsimd.memset(y_all[:], 0.0)
+        out_tiles = out.rearrange("(k p) q -> p k q", p=P)
+
+        def differences(k0, o_ps):
+            n = o_ps.shape[1]
+            y = y_all[:, k0 : k0 + n, :]
+            memory = memq_row[:, 1:Q].unsqueeze(1).to_broadcast([P, n, Q - 1])
+            nc.vector.tensor_tensor(out=y[:, :, 1:Q], in0=o_ps[:, :, 0 : Q - 1], in1=memory, op=ALU.mult)
             nc.vector.tensor_tensor(out=y, in0=o_ps[:], in1=y, op=ALU.subtract)
-            nc.sync.dma_start(out=out[k * P : (k + 1) * P, :], in_=y)
+            nc.sync.dma_start(out=out_tiles[:, k0 : k0 + n, :], in_=y)
 
-        sums = [product(k, sb.tile([P, P], U32, name="v_codes%d" % k, align_bytes=64)) for k in range(2)]
-        gathered.append(gather_values(3, "wt1"))
-        turned.append(turn_values(3, gathered[3]))
-        y_all = after_values(3, [P, 4, Q], F32, "y_all")
-        nc.vector.memset(y_all[:, :, 0:1], 0.0)
-        sums.append(product(2, after_values(3, [P, P], U32, "v_codes2", at=16 * Q)))
-        differences(0, sums[0])
-        differences(1, sums[1])
-        sums.append(product(3, sb.tile([P, P], U32, name="v_codes3", align_bytes=64)))
-        differences(2, sums[2])
-        differences(3, sums[3])
+        codes, scales = quantise(vt01[:].rearrange("p k i -> p (k i)"), shared("w1", [P, 2 * P], U32, "v_codes01")[:], "v_scales01")
+        o01 = bank(4, [P, 2, Q], "o_ps01")
+        for k in range(2):
+            product(o01[:, k, :], codes[:, k * P : (k + 1) * P], scales[:, k * P : (k + 1) * P])
+        o_late = []
+        for k in (2, 3):
+            v_codes = after_values(3, [P, P], U32, "v_codes%d" % k, at=4 * Q + 4 * P * (k - 2))
+            codes, scales = quantise(vt_late[k - 2][:], v_codes[:], "v_scales%d" % k)
+            o_ps = bank(4 + k, [P, 1, Q], "o_ps%d" % k)
+            product(o_ps[:, 0, :], codes, scales)
+            o_late.append(o_ps)
+        differences(0, o01)
+        differences(2, o_late[0])
+        differences(3, o_late[1])

@@ -6,6 +6,7 @@ from concourse.masks import make_identity
 D, T, I, Q, E, V = 512, 2048, 512, 256, 512, 32
 P = 128
 R = Q // V
+VALUE_TILE = (0, 2, 1, 3)
 FLOPS = 2 * D * I * Q + 2 * I * E * Q
 
 F32 = mybir.dt.float32
@@ -39,15 +40,15 @@ def tile_attend_groupbest_abstaining_rowchanges_kernel(
         lines = sb.tile([P, P], F32, name="lines")
         nc.gpsimd.memset(lines[:], 0.0)
 
-        offsets = sb.tile([P, I // 16], U16, name="offsets")
-        nc.sync.dma_start(offsets[:], offs)
-        q_raw = sb.tile([P, 4, Q], F32, name="q_raw")
-        nc.sync.dma_start(out=q_raw[:], in_=query.rearrange("(p t) q -> p t q", t=4))
         ks_rows = sb.tile([P, T // 4], I32, name="ks_rows")
         for g in range(4):
             rows = slice(32 * g, 32 * g + 4)
             nc.sync.dma_start(out=ks_rows[rows, :], in_=keys_scales[0, 4 * g : 4 * g + 4, :].bitcast(I32))
             nc.vector.tensor_copy(out=ks_pool[rows, :].bitcast(I32), in_=ks_rows[rows, :])
+        q_raw = sb.tile([P, 4, Q], F32, name="q_raw")
+        nc.sync.dma_start(out=q_raw[:], in_=query.rearrange("(p t) q -> p t q", t=4))
+        offsets = sb.tile([P, I // 16], U16, name="offsets")
+        nc.sync.dma_start(offsets[:], offs)
         k_pool = sb.tile([P, T], U32, name="k_pool")
         nc.sync.dma_start(out=k_pool[:].bitcast(I32), in_=keys_words[0].rearrange("p n t -> p (n t)").bitcast(I32))
         lam_col = sb.tile([P, 2], F32, name="lam_col")
@@ -62,11 +63,13 @@ def tile_attend_groupbest_abstaining_rowchanges_kernel(
 
         v_pool = [after_values(k, [P, T], F32, "v_pool%d" % k) for k in range(4)]
         nc.sync.dma_start(out=lines[0:4, :], in_=slot_factor.rearrange("o (c p) -> (o c) p", p=P))
-        nc.sync.dma_start(out=lines[4:6, :], in_=memq.rearrange("o (j p) -> (o j) p", p=P))
-        nc.sync.dma_start(out=lines[6:8, :], in_=eager.rearrange("(j p) o -> j (p o)", p=P))
-        nc.sync.dma_start(out=lines[8:10, :], in_=thresh.rearrange("(j p) o -> j (p o)", p=P))
+        nc.sync.dma_start(out=lines[4:6, :], in_=eager.rearrange("(j p) o -> j (p o)", p=P))
+        nc.sync.dma_start(out=lines[6:8, :], in_=thresh.rearrange("(j p) o -> j (p o)", p=P))
         for k in range(4):
-            nc.sync.dma_start(out=v_pool[k][:], in_=vals[k * P : (k + 1) * P, :])
+            rows = slice(VALUE_TILE[k] * P, (VALUE_TILE[k] + 1) * P)
+            nc.sync.dma_start(out=v_pool[k][:], in_=vals[rows, :])
+        memq_row = sb.tile([P, Q], F32, name="memq_row")
+        nc.sync.dma_start(out=memq_row[:], in_=memq[0].partition_broadcast(P))
 
         def columns(src, n, k, name):
             turned = bank(k, [P, P], name + "_ps")
@@ -141,8 +144,8 @@ def tile_attend_groupbest_abstaining_rowchanges_kernel(
             for c in range(4):
                 turn(c, j, t_sb[j][:, c, :], False, c == 3)
 
-        cols = columns(lines, 10, 7, "cols")
-        os_col, memq_col, eager_col, thresh_col = cols[:, 0:4], cols[:, 4:6], cols[:, 6:8], cols[:, 8:10]
+        cols = columns(lines, 8, 7, "cols")
+        os_col, eager_col, thresh_col = cols[:, 0:4], cols[:, 4:6], cols[:, 6:8]
         os_row = bank(6, [P, I], "os_row")
         spread(os_row, os_col, 4)
 
@@ -157,6 +160,10 @@ def tile_attend_groupbest_abstaining_rowchanges_kernel(
             nc.scalar.copy(out=dst_bf.bitcast(F32).rearrange("p (x u) -> p x u", u=2), in_=psum_tile[:].rearrange("p u x -> p x u"))
 
         g0_bf = gather_values(0, shared("g0", [P, I], BF16, "g0_bf"))
+        v1_bf = shared("v1_bf", [P, T], BF16, "v1_bf")
+        for n in range(4):
+            part = slice(n * T // 4, (n + 1) * T // 4)
+            nc.gpsimd.tensor_copy(out=v1_bf[:, part], in_=v_pool[1][:, part])
 
         p_sb, shift = [], []
         for j in range(2):
@@ -176,18 +183,19 @@ def tile_attend_groupbest_abstaining_rowchanges_kernel(
             nc.vector.tensor_reduce(out=neg_max, in_=s_ps[j][:], axis=AX.X, op=ALU.max, negate=True)
             odds = shared("odds%d" % j, [P, 1], F32, "odds%d" % j)
             nc.scalar.activation(out=odds[:], in_=neg_max, func=ACT.Exp, scale=eager_col[:, j : j + 1], bias=shift[j][:])
-            p_sum = sb.tile([P, 1], F32, name="p_sum%d" % j)
+            p_sum = shared("p_sum%d" % j, [P, 1], F32, "p_sum%d" % j)
             nc.scalar.activation(out=p_sb[j][:], in_=s_ps[j][:], func=ACT.Exp, bias=neg_max, scale=1.0, accum_out=p_sum[:])
             d = sb.tile([P, 1], F32, name="denom%d" % j)
             nc.scalar.activation(out=d[:], in_=odds[:], func=ACT.Identity, scale=p_sum[:], bias=p_sum[:])
             denom.append(d)
-        g1_bf = gather_values(1, shared("shift0", [P, I], BF16, "g1_bf"))
-        vt01 = shared("odds1", [P, 2, I], BF16, "vt01")
-        for k, g_bf in enumerate((g0_bf, g1_bf)):
-            turn_pairs(g_bf[:], bank(2, [P, 2, P], "vt_ps%d" % k), vt01[:, k, :])
+        g2_bf = gather_values(2, shared("shift0", [P, I], BF16, "g2_bf"))
+        vt_a = shared("odds1", [P, 2, I], BF16, "vt_a")
+        turn_pairs(g0_bf[:], bank(2, [P, 2, P], "vt_ps0"), vt_a[:, 0, :])
+        g1_bf = shared("p_sum1", [P, I], BF16, "g1_bf")
+        nc.scalar.activation(out=g1_bf[:], in_=v1_bf[:].indirect(offsets[:]), func=ACT.Copy)
 
-        row_factor = after_values(1, [P, 2], F32, "row_factor")
-        wt_bf = []
+        row_factor = after_values(2, [P, 2], F32, "row_factor")
+        wt_bf = shared("v1_bf", [P, 2, I], BF16, "wt_bf")
         for j in range(2):
             factor = row_factor[:, j : j + 1]
             nc.vector.reciprocal(out=factor, in_=denom[j][:])
@@ -195,65 +203,46 @@ def tile_attend_groupbest_abstaining_rowchanges_kernel(
             nc.vector.scalar_tensor_tensor(
                 out=w_bf[:], in0=p_sb[j][:], scalar=factor, in1=os_row[:], op0=ALU.mult, op1=ALU.mult
             )
-            wt = sb.tile([P, I], BF16, name="wt_bf%d" % j, align_bytes=64)
-            turn_pairs(w_bf[:], bank(j, [P, 2, P], "wt_ps%d" % j), wt[:])
-            wt_bf.append(wt)
-        memq_ps = bank(5, [P, Q], "memq_ps")
-        spread(memq_ps, memq_col, 2)
-        memq_row = sb.tile([P, Q], F32, name="memq_row")
-        nc.scalar.copy(out=memq_row[:], in_=memq_ps[:])
-        vt_late = []
-        for k in (2, 3):
-            g_bf = gather_values(k, after_values(4, [P, I], BF16, "g%d_bf" % k, at=4 * I + 2 * I * (k - 2)))
-            vt = sb.tile([P, I], BF16, name="vt%d" % k, align_bytes=64)
-            turn_pairs(g_bf[:], bank(k - 2, [P, 2, P], "vt_ps%d" % k), vt[:])
-            vt_late.append(vt)
+            turn_pairs(w_bf[:], bank(j, [P, 2, P], "wt_ps%d" % j), wt_bf[:, j, :])
+        g3_bf = gather_values(3, after_values(4, [P, I], BF16, "g3_bf", at=4 * I))
+        turn_pairs(g2_bf[:], bank(0, [P, 2, P], "vt_ps2"), vt_a[:, 1, :])
+        vt_b = shared("vt23", [P, 2, I], BF16, "vt_b")
+        turn_pairs(g1_bf[:], bank(1, [P, 2, P], "vt_ps1"), vt_b[:, 0, :])
+        turn_pairs(g3_bf[:], bank(3, [P, 2, P], "vt_ps3"), vt_b[:, 1, :])
 
-        def quantise(src_bf, codes, name):
-            scales = sb.tile([P, codes.shape[1]], U8, name=name, align_bytes=64)
-            nc.vector.quantize_mx(out=codes.bitcast(FP8X4), scales=scales[:], in_=src_bf)
-            return codes, scales[:]
+        def quantise(src_bf, n, name):
+            codes = after_values(3, [P, Q], U32, name + "_codes", at=4 * Q * n)
+            scales = sb.tile([P, Q], U8, name=name + "_scales", align_bytes=64)
+            nc.vector.quantize_mx(out=codes[:].bitcast(FP8X4), scales=scales[:], in_=src_bf[:].rearrange("p k i -> p (k i)"))
+            return codes, scales
 
-        w_codes = after_values(3, [P, Q], U32, "w_codes")
-        w_scales = sb.tile([P, Q], U8, name="w_scales", align_bytes=64)
-        for j in range(2):
-            qs = slice(j * P, (j + 1) * P)
-            nc.vector.quantize_mx(out=w_codes[:, qs].bitcast(FP8X4), scales=w_scales[:, qs], in_=wt_bf[j][:])
+        w_codes, w_scales = quantise(wt_bf, 0, "w")
 
-        def product(o_ps, v_codes, v_scales):
-            nc.tensor.matmul_mx(
-                out=o_ps,
-                lhsT=v_codes.bitcast(FP8X4),
-                lhsT_scale=v_scales,
-                rhs=w_codes[:].bitcast(FP8X4),
-                rhs_scale=w_scales[:],
-                start=True,
-                stop=True,
-            )
+        carry = sb.tile([P, 4, Q], F32, name="carry")
+        nc.gpsimd.memset(carry[:, :, 0:8], 0.0)
+        memory = memq_row[:, 1:Q].unsqueeze(1).to_broadcast([P, 2, Q - 1])
 
-        y_all = sb.tile([P, 4, Q], F32, name="y_all")
-        nc.gpsimd.memset(y_all[:], 0.0)
-        out_tiles = out.rearrange("(k p) q -> p k q", p=P)
+        def product(pair, vt):
+            v_codes, v_scales = quantise(vt, 1 + pair, "v%d" % pair)
+            o_ps = bank(4 + 2 * pair, [P, 2, Q], "o_ps%d" % pair)
+            for h in range(2):
+                nc.tensor.matmul_mx(
+                    out=o_ps[:, h, :],
+                    lhsT=v_codes[:, h * P : (h + 1) * P].bitcast(FP8X4),
+                    lhsT_scale=v_scales[:, h * P : (h + 1) * P],
+                    rhs=w_codes[:].bitcast(FP8X4),
+                    rhs_scale=w_scales[:],
+                    start=True,
+                    stop=True,
+                )
+            return o_ps
 
-        def differences(k0, o_ps):
-            n = o_ps.shape[1]
-            y = y_all[:, k0 : k0 + n, :]
-            memory = memq_row[:, 1:Q].unsqueeze(1).to_broadcast([P, n, Q - 1])
-            nc.vector.tensor_tensor(out=y[:, :, 1:Q], in0=o_ps[:, :, 0 : Q - 1], in1=memory, op=ALU.mult)
-            nc.vector.tensor_tensor(out=y, in0=o_ps[:], in1=y, op=ALU.subtract)
-            nc.sync.dma_start(out=out_tiles[:, k0 : k0 + n, :], in_=y)
-
-        codes, scales = quantise(vt01[:].rearrange("p k i -> p (k i)"), shared("w1", [P, 2 * P], U32, "v_codes01")[:], "v_scales01")
-        o01 = bank(4, [P, 2, Q], "o_ps01")
-        for k in range(2):
-            product(o01[:, k, :], codes[:, k * P : (k + 1) * P], scales[:, k * P : (k + 1) * P])
-        o_late = []
-        for k in (2, 3):
-            v_codes = after_values(3, [P, P], U32, "v_codes%d" % k, at=4 * Q + 4 * P * (k - 2))
-            codes, scales = quantise(vt_late[k - 2][:], v_codes[:], "v_scales%d" % k)
-            o_ps = bank(4 + k, [P, 1, Q], "o_ps%d" % k)
-            product(o_ps[:, 0, :], codes, scales)
-            o_late.append(o_ps)
-        differences(0, o01)
-        differences(2, o_late[0])
-        differences(3, o_late[1])
+        sums = [product(0, vt_a), product(1, vt_b)]
+        for pair, o_ps in enumerate(sums):
+            tiles = slice(2 * pair, 2 * pair + 2)
+            nc.vector.tensor_tensor(out=carry[:, tiles, 1:Q], in0=o_ps[:, :, 0 : Q - 1], in1=memory, op=ALU.mult)
+            y = shared(("vt23", "y23")[pair], [P, 2, Q], F32, "y%d" % pair)
+            for h in range(2):
+                k = 2 * pair + h
+                nc.vector.tensor_tensor(out=y[:, h, :], in0=o_ps[:, h, :], in1=carry[:, k, :], op=ALU.subtract)
+                nc.sync.dma_start(out=out[k * P : (k + 1) * P, :], in_=y[:, h, :])

@@ -206,13 +206,15 @@ def tile_attend_groupbest_abstaining_rowchanges_kernel(
             turn_pairs(w_bf[:], bank(j, [P, 2, P], "wt_ps%d" % j), wt_bf[:, j, :])
         g3_bf = gather_values(3, after_values(4, [P, I], BF16, "g3_bf", at=4 * I))
         turn_pairs(g2_bf[:], bank(0, [P, 2, P], "vt_ps2"), vt_a[:, 1, :])
-        vt_b = shared("vt23", [P, 2, I], BF16, "vt_b")
+        vt_b = sb.tile([P, 1, I], BF16, name="vt_b", align_bytes=64)
         turn_pairs(g1_bf[:], bank(1, [P, 2, P], "vt_ps1"), vt_b[:, 0, :])
-        turn_pairs(g3_bf[:], bank(3, [P, 2, P], "vt_ps3"), vt_b[:, 1, :])
+        vt_c = shared("vt_c", [P, 1, I], BF16, "vt_c")
+        turn_pairs(g3_bf[:], bank(3, [P, 2, P], "vt_ps3"), vt_c[:, 0, :])
 
         def quantise(src_bf, n, name):
-            codes = after_values(3, [P, Q], U32, name + "_codes", at=4 * Q * n)
-            scales = sb.tile([P, Q], U8, name=name + "_scales", align_bytes=64)
+            width = src_bf.shape[1] * P
+            codes = after_values(3, [P, width], U32, name + "_codes", at=4 * Q * n)
+            scales = sb.tile([P, width], U8, name=name + "_scales", align_bytes=64)
             nc.vector.quantize_mx(out=codes[:].bitcast(FP8X4), scales=scales[:], in_=src_bf[:].rearrange("p k i -> p (k i)"))
             return codes, scales
 
@@ -220,29 +222,34 @@ def tile_attend_groupbest_abstaining_rowchanges_kernel(
 
         carry = sb.tile([P, 4, Q], F32, name="carry")
         nc.gpsimd.memset(carry[:, :, 0:8], 0.0)
-        memory = memq_row[:, 1:Q].unsqueeze(1).to_broadcast([P, 2, Q - 1])
 
-        def product(pair, vt):
-            v_codes, v_scales = quantise(vt, 1 + pair, "v%d" % pair)
-            o_ps = bank(4 + 2 * pair, [P, 2, Q], "o_ps%d" % pair)
-            for h in range(2):
-                nc.tensor.matmul_mx(
-                    out=o_ps[:, h, :],
-                    lhsT=v_codes[:, h * P : (h + 1) * P].bitcast(FP8X4),
-                    lhsT_scale=v_scales[:, h * P : (h + 1) * P],
-                    rhs=w_codes[:].bitcast(FP8X4),
-                    rhs_scale=w_scales[:],
-                    start=True,
-                    stop=True,
-                )
+        def product(k, v_codes, v_scales):
+            o_ps = bank(4 + k, [P, Q], "o_ps%d" % k)
+            nc.tensor.matmul_mx(
+                out=o_ps[:],
+                lhsT=v_codes.bitcast(FP8X4),
+                lhsT_scale=v_scales,
+                rhs=w_codes[:].bitcast(FP8X4),
+                rhs_scale=w_scales[:],
+                start=True,
+                stop=True,
+            )
             return o_ps
 
-        sums = [product(0, vt_a), product(1, vt_b)]
-        for pair, o_ps in enumerate(sums):
-            tiles = slice(2 * pair, 2 * pair + 2)
-            nc.vector.tensor_tensor(out=carry[:, tiles, 1:Q], in0=o_ps[:, :, 0 : Q - 1], in1=memory, op=ALU.mult)
-            y = shared(("vt23", "y23")[pair], [P, 2, Q], F32, "y%d" % pair)
-            for h in range(2):
-                k = 2 * pair + h
-                nc.vector.tensor_tensor(out=y[:, h, :], in0=o_ps[:, h, :], in1=carry[:, k, :], op=ALU.subtract)
-                nc.sync.dma_start(out=out[k * P : (k + 1) * P, :], in_=y[:, h, :])
+        def differences(engine, k, o, y):
+            engine.tensor_tensor(out=carry[:, k, 1:Q], in0=o[:, 0 : Q - 1], in1=memq_row[:, 1:Q], op=ALU.mult)
+            engine.tensor_tensor(out=y[:], in0=o[:], in1=carry[:, k, :], op=ALU.subtract)
+            nc.sync.dma_start(out=out[k * P : (k + 1) * P, :], in_=y[:])
+
+        codes, scales = quantise(vt_a, 1, "va")
+        sums = [product(k, codes[:, k * P : (k + 1) * P], scales[:, k * P : (k + 1) * P]) for k in range(2)]
+        for k, vt in ((2, vt_b), (3, vt_c)):
+            codes, scales = quantise(vt, k, "v%d" % k)
+            sums.append(product(k, codes[:], scales[:]))
+
+        o0 = sb.tile([P, Q], F32, name="o0")
+        nc.scalar.copy(out=o0[:], in_=sums[0][:])
+        differences(nc.gpsimd, 0, o0, sb.tile([P, Q], F32, name="y0"))
+        differences(nc.vector, 1, sums[1], shared("vt_c", [P, Q], F32, "y1"))
+        for k in (2, 3):
+            differences(nc.vector, k, sums[k], sb.tile([P, Q], F32, name="y%d" % k))

from contextlib import ExitStack

import concourse.mybir as mybir
from concourse.masks import make_identity

D, T, I, Q, E, V = 512, 2048, 512, 256, 512, 32
P = 128
R = Q // V
VALUE_TILE = (0, 2, 1, 3)
FLOPS = 2 * D * I * Q + 2 * I * E * Q

F32 = mybir.dt.float32
BF16 = mybir.dt.bfloat16
I32 = mybir.dt.int32
U32 = mybir.dt.uint32
U16 = mybir.dt.uint16
U8 = mybir.dt.uint8
FP8X4 = mybir.dt.float8_e4m3fn_x4
ALU = mybir.AluOpType
ACT = mybir.ActivationFunctionType
AX = mybir.AxisListType


def tile_attend_groupbest_abstaining_rowchanges_kernel(
    tc, query, keys_words, keys_scales, lam, eager, thresh, slot_factor, vals, memq, offs, out
):
    nc = tc.nc
    with ExitStack() as ctx:
        sb = ctx.enter_context(tc.tile_pool(name="sb", bufs=1))
        reuse = ctx.enter_context(tc.tile_pool(name="reuse", bufs=1))
        ps = ctx.enter_context(tc.psum_pool(name="ps", bufs=1))

        def bank(k, shape, name):
            return ps.tile(shape, F32, name=name, tag="bank%d" % k)

        ks_pool = sb.tile([P, T], U8, name="ks_pool")
        nc.vector.memset(ks_pool[:].bitcast(I32), 0)
        ident = sb.tile([P, P], F32, name="ident")
        make_identity(nc, ident[:])
        lines = sb.tile([P, P], F32, name="lines")
        nc.gpsimd.memset(lines[:], 0.0)

        ks_rows = sb.tile([P, T // 4], I32, name="ks_rows")
        for g in range(4):
            rows = slice(32 * g, 32 * g + 4)
            nc.sync.dma_start(out=ks_rows[rows, :], in_=keys_scales[0, 4 * g : 4 * g + 4, :].bitcast(I32))
            nc.vector.tensor_copy(out=ks_pool[rows, :].bitcast(I32), in_=ks_rows[rows, :])
        q_raw = sb.tile([P, 4, Q], F32, name="q_raw")
        nc.sync.dma_start(out=q_raw[:], in_=query.rearrange("(p t) q -> p t q", t=4))
        offsets = sb.tile([P, I // 16], U16, name="offsets")
        nc.sync.dma_start(offsets[:], offs)
        k_pool = sb.tile([P, T], U32, name="k_pool")
        nc.sync.dma_start(out=k_pool[:].bitcast(I32), in_=keys_words[0].rearrange("p n t -> p (n t)").bitcast(I32))
        lam_col = sb.tile([P, 2], F32, name="lam_col")
        with nc.allow_non_contiguous_dma(reason="one value of lam to each partition"):
            nc.sync.dma_start(out=lam_col[:], in_=lam.rearrange("o (j p) -> p (o j)", p=P))

        def after_values(k, shape, dtype, name, at=0):
            return reuse.tile(shape, dtype, name=name, offset=4 * T * k + at, align_bytes=64)

        def shared(tag, shape, dtype, name):
            return sb.tile(shape, dtype, name=name, tag=tag, align_bytes=64)

        v_pool = [after_values(k, [P, T], F32, "v_pool%d" % k) for k in range(4)]
        nc.sync.dma_start(out=lines[0:4, :], in_=slot_factor.rearrange("o (c p) -> (o c) p", p=P))
        nc.sync.dma_start(out=lines[4:6, :], in_=eager.rearrange("(j p) o -> j (p o)", p=P))
        nc.sync.dma_start(out=lines[6:8, :], in_=thresh.rearrange("(j p) o -> j (p o)", p=P))
        for k in range(4):
            rows = slice(VALUE_TILE[k] * P, (VALUE_TILE[k] + 1) * P)
            nc.sync.dma_start(out=v_pool[k][:], in_=vals[rows, :])
        memq_row = sb.tile([P, Q], F32, name="memq_row")
        nc.sync.dma_start(out=memq_row[:], in_=memq[0].partition_broadcast(P))

        def columns(src, n, k, name):
            turned = bank(k, [P, P], name + "_ps")
            nc.tensor.transpose(turned[:], src[:], ident[:])
            col = sb.tile([P, n], F32, name=name)
            nc.scalar.activation(out=col[:], in_=turned[:, 0:n], func=ACT.Copy)
            return col

        def spread(dst, col, n):
            for j in range(n):
                nc.tensor.transpose(dst[:, j * P : (j + 1) * P], col[:, j : j + 1].to_broadcast([P, P]), ident[:])


        q_bf = sb.tile([P, Q, 4], BF16, name="q_bf", align_bytes=64)
        nc.scalar.activation(out=q_bf[:], in_=q_raw[:].rearrange("p t q -> p q t"), func=ACT.Copy)
        q_codes = sb.tile([P, Q], U32, name="q_codes", align_bytes=64)
        q_scales = sb.tile([P, Q], U8, name="q_scales", align_bytes=64)
        nc.vector.quantize_mx(out=q_codes[:].bitcast(FP8X4), scales=q_scales[:], in_=q_bf[:].rearrange("p q t -> p (q t)"))

        ks = sb.tile([P, I], U8, name="ks", align_bytes=64)
        nc.vector.tensor_copy(out=ks[:], in_=ks_pool[:].indirect(offsets[:]))
        kw = []
        for b in range(2):
            w = sb.tile([P, 2 * P], U32, name="kw%d" % b, align_bytes=64)
            nc.vector.tensor_copy(out=w[:], in_=k_pool[:].indirect(offsets[:, 16 * b : 16 * (b + 1)]))
            kw.append(w)

        a_ps = []
        for c in range(4):
            acc = bank(c, [P, Q], "a_ps%d" % c)
            nc.tensor.matmul_mx(
                out=acc[:],
                lhsT=kw[c // 2][:, (c % 2) * P : (c % 2 + 1) * P].bitcast(FP8X4),
                lhsT_scale=ks[:, c * P : (c + 1) * P],
                rhs=q_codes[:].bitcast(FP8X4),
                rhs_scale=q_scales[:],
                start=True,
                stop=True,
            )
            a_ps.append(acc)
        lam_row = bank(6, [P, Q], "lam_row")
        spread(lam_row, lam_col, 2)
        a_sb = []
        neg_best = shared("g0", [P, 4, V], F32, "neg_best")
        for c in range(4):
            nc.vector.tensor_reduce(
                out=neg_best[:, c, :], in_=a_ps[c][:].rearrange("p (v r) -> p v r", r=R), axis=AX.X, op=ALU.max, negate=True
            )
            a = sb.tile([P, Q], F32, name="a_sb%d" % c)
            nc.scalar.copy(out=a[:], in_=a_ps[c][:])
            a_sb.append(a)
        VJ = V // 2
        t_sb = []
        for j in range(2):
            t = sb.tile([P, 4, P], F32, name="t_sb%d" % j)
            nc.vector.tensor_tensor(
                out=t[:].rearrange("p c (v r) -> p c v r", r=R),
                in0=neg_best[:, :, j * VJ : (j + 1) * VJ].unsqueeze(3).to_broadcast([P, 4, VJ, R]),
                in1=lam_row[:, j * P : (j + 1) * P].rearrange("p (v r) -> p v r", r=R).unsqueeze(1).to_broadcast([P, 4, VJ, R]),
                op=ALU.mult,
            )
            t_sb.append(t)

        s_ps = [bank(4 + j, [P, I], "s_ps%d" % j) for j in range(2)]

        def turn(c, j, src, start, stop):
            nc.tensor.matmul(s_ps[j][:, c * P : (c + 1) * P], src, ident[:], start=start, stop=stop, is_transpose=True)

        for j in range(2):
            for c in range(4):
                turn(c, j, a_sb[c][:, j * P : (j + 1) * P], c == 0, False)
            for c in range(4):
                turn(c, j, t_sb[j][:, c, :], False, c == 3)

        cols = columns(lines, 8, 7, "cols")
        os_col, eager_col, thresh_col = cols[:, 0:4], cols[:, 4:6], cols[:, 6:8]
        os_row = bank(6, [P, I], "os_row")
        spread(os_row, os_col, 4)

        def gather_values(k, g_bf):
            nc.vector.tensor_copy(out=g_bf[:], in_=v_pool[k][:].indirect(offsets[:]))
            return g_bf

        def turn_pairs(src_bf, psum_tile, dst_bf):
            words = src_bf.bitcast(F32)
            for u in range(2):
                nc.tensor.transpose(psum_tile[:, u, :], words[:, u : 2 * P : 2], ident[:])
            nc.scalar.copy(out=dst_bf.bitcast(F32).rearrange("p (x u) -> p x u", u=2), in_=psum_tile[:].rearrange("p u x -> p x u"))

        g0_bf = gather_values(0, shared("g0", [P, I], BF16, "g0_bf"))
        v1_bf = shared("v1_bf", [P, T], BF16, "v1_bf")
        for n in range(4):
            part = slice(n * T // 4, (n + 1) * T // 4)
            nc.gpsimd.tensor_copy(out=v1_bf[:, part], in_=v_pool[1][:, part])

        p_sb, shift = [], []
        for j in range(2):
            p = after_values(4, [P, I], F32, "p_sb%d" % j, at=4 * I * j)
            mean = sb.tile([P, 1], F32, name="mean%d" % j)
            nc.scalar.activation(out=p[:], in_=s_ps[j][:], func=ACT.Copy, scale=1.0 / I, accum_out=mean[:])
            sh = shared("shift%d" % j, [P, 1], F32, "shift%d" % j)
            nc.scalar.activation(
                out=sh[:], in_=mean[:], func=ACT.Identity, scale=eager_col[:, j : j + 1], bias=thresh_col[:, j : j + 1]
            )
            p_sb.append(p)
            shift.append(sh)
        row_max = after_values(0, [P, 2], F32, "row_max")
        denom = []
        for j in range(2):
            neg_max = row_max[:, j : j + 1]
            nc.vector.tensor_reduce(out=neg_max, in_=s_ps[j][:], axis=AX.X, op=ALU.max, negate=True)
            odds = shared("odds%d" % j, [P, 1], F32, "odds%d" % j)
            nc.scalar.activation(out=odds[:], in_=neg_max, func=ACT.Exp, scale=eager_col[:, j : j + 1], bias=shift[j][:])
            p_sum = shared("p_sum%d" % j, [P, 1], F32, "p_sum%d" % j)
            nc.scalar.activation(out=p_sb[j][:], in_=s_ps[j][:], func=ACT.Exp, bias=neg_max, scale=1.0, accum_out=p_sum[:])
            d = sb.tile([P, 1], F32, name="denom%d" % j)
            nc.scalar.activation(out=d[:], in_=odds[:], func=ACT.Identity, scale=p_sum[:], bias=p_sum[:])
            denom.append(d)
        g2_bf = gather_values(2, shared("shift0", [P, I], BF16, "g2_bf"))
        vt_a = shared("odds1", [P, 2, I], BF16, "vt_a")
        turn_pairs(g0_bf[:], bank(2, [P, 2, P], "vt_ps0"), vt_a[:, 0, :])
        g1_bf = shared("p_sum1", [P, I], BF16, "g1_bf")
        nc.scalar.activation(out=g1_bf[:], in_=v1_bf[:].indirect(offsets[:]), func=ACT.Copy)

        row_factor = after_values(2, [P, 2], F32, "row_factor")
        wt_bf = shared("v1_bf", [P, 2, I], BF16, "wt_bf")
        for j in range(2):
            factor = row_factor[:, j : j + 1]
            nc.vector.reciprocal(out=factor, in_=denom[j][:])
            w_bf = shared("w%d" % j, [P, I], BF16, "w_bf%d" % j)
            nc.vector.scalar_tensor_tensor(
                out=w_bf[:], in0=p_sb[j][:], scalar=factor, in1=os_row[:], op0=ALU.mult, op1=ALU.mult
            )
            turn_pairs(w_bf[:], bank(j, [P, 2, P], "wt_ps%d" % j), wt_bf[:, j, :])
        g3_bf = gather_values(3, after_values(4, [P, I], BF16, "g3_bf", at=4 * I))
        turn_pairs(g2_bf[:], bank(0, [P, 2, P], "vt_ps2"), vt_a[:, 1, :])
        vt_b = sb.tile([P, 1, I], BF16, name="vt_b", align_bytes=64)
        turn_pairs(g1_bf[:], bank(1, [P, 2, P], "vt_ps1"), vt_b[:, 0, :])
        vt_c = shared("vt_c", [P, 1, I], BF16, "vt_c")
        turn_pairs(g3_bf[:], bank(3, [P, 2, P], "vt_ps3"), vt_c[:, 0, :])

        def quantise(src_bf, n, name):
            width = src_bf.shape[1] * P
            codes = after_values(3, [P, width], U32, name + "_codes", at=4 * Q * n)
            scales = sb.tile([P, width], U8, name=name + "_scales", align_bytes=64)
            nc.vector.quantize_mx(out=codes[:].bitcast(FP8X4), scales=scales[:], in_=src_bf[:].rearrange("p k i -> p (k i)"))
            return codes, scales

        w_codes, w_scales = quantise(wt_bf, 0, "w")

        carry = sb.tile([P, 4, Q], F32, name="carry")
        nc.gpsimd.memset(carry[:, :, 0:8], 0.0)

        def product(k, v_codes, v_scales):
            o_ps = bank(4 + k, [P, Q], "o_ps%d" % k)
            nc.tensor.matmul_mx(
                out=o_ps[:],
                lhsT=v_codes.bitcast(FP8X4),
                lhsT_scale=v_scales,
                rhs=w_codes[:].bitcast(FP8X4),
                rhs_scale=w_scales[:],
                start=True,
                stop=True,
            )
            return o_ps

        def differences(engine, k, o, y):
            engine.tensor_tensor(out=carry[:, k, 1:Q], in0=o[:, 0 : Q - 1], in1=memq_row[:, 1:Q], op=ALU.mult)
            engine.tensor_tensor(out=y[:], in0=o[:], in1=carry[:, k, :], op=ALU.subtract)
            nc.sync.dma_start(out=out[k * P : (k + 1) * P, :], in_=y[:])

        codes, scales = quantise(vt_a, 1, "va")
        sums = [product(k, codes[:, k * P : (k + 1) * P], scales[:, k * P : (k + 1) * P]) for k in range(2)]
        for k, vt in ((2, vt_b), (3, vt_c)):
            codes, scales = quantise(vt, k, "v%d" % k)
            sums.append(product(k, codes[:], scales[:]))

        o0 = sb.tile([P, Q], F32, name="o0")
        nc.scalar.copy(out=o0[:], in_=sums[0][:])
        differences(nc.gpsimd, 0, o0, sb.tile([P, Q], F32, name="y0"))
        differences(nc.vector, 1, sums[1], shared("vt_c", [P, Q], F32, "y1"))
        for k in (2, 3):
            differences(nc.vector, k, sums[k], sb.tile([P, Q], F32, name="y%d" % k))
